import numpy as np
import ml_dtypes


def mxq(x, axis, fmt="e4m3"):
    dtype, down = {"e4m3": (ml_dtypes.float8_e4m3fn, 7), "e5m2": (ml_dtypes.float8_e5m2, 14)}[fmt]
    v = np.moveaxis(np.asarray(x, np.float32).astype(ml_dtypes.bfloat16).astype(np.float64), axis, -1)
    blocks = v.reshape(v.shape[:-1] + (-1, 32))
    amax = np.abs(blocks).max(-1, keepdims=True)
    byte = np.maximum(np.where(amax > 0, np.frexp(amax)[1] - 1 + 127, 0) - down, 1)
    scale = np.exp2(byte - 127.0)
    codes = (blocks / scale).astype(np.float32).astype(dtype).astype(np.float64)
    return np.moveaxis((codes * scale).reshape(v.shape), -1, axis)


WIDE = False


def mx_kscale(k):
    if not WIDE:
        return np.ones(k)
    levels = np.array([10, -10, 5, -5, 0])
    if k % 512:
        return np.exp2(np.random.permutation(np.resize(levels, k // 32))).repeat(32)
    a = np.empty((k // 512, 16))
    for p in range(k // 512):
        a[p, :8] = np.random.permutation(np.resize(levels, 8))
        for g in range(8):
            far = levels[np.abs(levels - a[p, g]) >= 10]
            a[p, g + 8] = far[np.random.randint(len(far))]
    return np.exp2(a.ravel()).repeat(32)


BF16 = ml_dtypes.bfloat16


def bf(x):
    return np.asarray(x, np.float32).astype(BF16)


def f64(x):
    return np.asarray(x).astype(np.float64)


E2M1 = np.array([0.0, 0.5, 1.0, 1.5, 2.0, 3.0, 4.0, 6.0, -0.0, -0.5, -1.0, -1.5, -2.0, -3.0, -4.0, -6.0])


def pack_weight(w, fmt):
    k, n = w.shape
    w = f64(bf(w)).reshape(k // 32, 32, n)
    amax = np.abs(w).max(1)
    if fmt == "e4m3":
        byte = np.frexp(amax)[1] - 1 + 127 - 7
    else:
        mant, ex = np.frexp(amax / 6.0)
        byte = np.where(mant > 0.5, ex, ex - 1) + 127
    byte = np.clip(np.where(amax > 0, byte, 1), 1, 254)
    scaled = (w * np.exp2(127.0 - byte)[:, None, :]).reshape(k, n).astype(np.float32)
    by_word = np.ascontiguousarray(scaled.reshape(k // 512, 128, 4, n).transpose(0, 1, 3, 2))
    if fmt == "e4m3":
        words = by_word.astype(ml_dtypes.float8_e4m3fn).view(np.uint8)
    else:
        c = by_word.astype(ml_dtypes.float4_e2m1fn).view(np.uint8) & 0xF
        words = c[..., 0::2] | (c[..., 1::2] << 4)
    return np.ascontiguousarray(words), np.ascontiguousarray(byte.astype(np.uint8).reshape(k // 512, 16, n))


def unpack_weight(words, scales, fmt):
    g, p, n, _ = words.shape
    if fmt == "e4m3":
        vals = np.ascontiguousarray(words).view(ml_dtypes.float8_e4m3fn).astype(np.float64)
    else:
        nib = np.empty((g, p, n, 4), np.uint8)
        nib[..., 0::2] = words & 0xF
        nib[..., 1::2] = words >> 4
        vals = E2M1[nib]
    vals = vals * np.repeat(np.exp2(scales.astype(np.float64) - 127.0), 8, axis=1)[..., None]
    return vals.transpose(0, 1, 3, 2).reshape(g * 512, n)
def pack4(w):
    words, scales = pack_weight(w, "e2m1")
    return words.reshape(words.shape[0], 128, -1), scales


def unpack4(words, scales):
    return unpack_weight(words.reshape(words.shape[0], 128, -1, 2), scales, "e2m1")


def planes(Y):
    n, m = Y.shape
    b = f64(bf(Y)).reshape(n // 32, 32, m)
    amax = np.abs(b).max(1)
    byte = np.clip(np.where(amax > 0, np.frexp(amax)[1] - 1 + 127 - 7, 1), 1, 254)
    codes = (b * np.exp2(127.0 - byte)[:, None, :]).reshape(n, m).astype(np.float32).astype(ml_dtypes.float8_e4m3fn).view(np.uint8)
    words = codes.reshape(n // 512, 128, 4, m).transpose(0, 1, 3, 2)
    return np.ascontiguousarray(words), np.ascontiguousarray(byte.astype(np.uint8).reshape(n // 512, 16, m))


V, C = 1536, 512

HALF = 0.5
LABEL_STD = 0.3


def setup_inputs():
    s = mx_kscale(V)
    t = mx_kscale(V)
    u = np.random.randn(V, V)
    a = (u + u.T) / np.sqrt(2.0) * V ** -0.25 * (1.0 - np.eye(V))
    adj4_words, adj4_scales = pack4(a / s[:, None] * (t / s)[None, :])
    labels = LABEL_STD * np.random.randn(V, C)
    lab_words, lab_scales = pack4(labels / t[:, None])
    spread = np.exp(0.8 * np.random.randn(C))
    compat = spread[None, :] * np.exp(0.3 * np.random.randn(V, C))
    return {"adj": bf(a * s[None, :]),
            "adj4_words": adj4_words, "adj4_scales": adj4_scales,
            "lab_words": lab_words, "lab_scales": lab_scales,
            "compat": bf(compat)}


def reference(adj, adj4_words, adj4_scales, lab_words, lab_scales, compat):
    A = f64(adj)
    B = unpack4(adj4_words, adj4_scales)
    L = unpack4(lab_words, lab_scales)
    P = mxq(A, 1, "e4m3") @ B
    H = P * A
    S = mxq(H, 1, "e4m3") @ L
    y = HALF * S * f64(compat)
    Y = y.T
    words, scales = planes(Y)
    return y, words, scales

@@ -1,0 +1,293 @@
+from contextlib import ExitStack
+
+import concourse.mybir as mybir
+from concourse.masks import make_identity
+
+V, C = 1536, 512
+FLOPS = 2 * V * V * (V + C)
+
+F32 = mybir.dt.float32
+BF16 = mybir.dt.bfloat16
+I32 = mybir.dt.int32
+U32 = mybir.dt.uint32
+U8 = mybir.dt.uint8
+FP8X4 = mybir.dt.float8_e4m3fn_x4
+FP4X4 = mybir.dt.float4_e2m1fn_x4
+MULT = mybir.AluOpType.mult
+
+P = 128
+K_PASS = 512
+GROUPS = V // K_PASS
+TILES = V // P
+RING = 3
+R_BATCH = 4
+HALF = 0.5
+
+
+def tile_triangle_label_scores_h1_kernel(
+    tc, adj, adj4_words, adj4_scales, lab_words, lab_scales, compat, out_0, out_1, out_2
+):
+    nc = tc.nc
+    with ExitStack() as ctx:
+        sb = ctx.enter_context(tc.tile_pool(name="sb", bufs=1))
+        ps = ctx.enter_context(tc.psum_pool(name="ps", bufs=1))
+
+        def sbuf(name, shape, dtype):
+            return sb.tile(shape, dtype, name=name, align_bytes=64)
+
+        def ring(name, shape, dtype):
+            return [sbuf("%s%d" % (name, k), shape, dtype) for k in range(RING)]
+
+        ident = sbuf("ident", [P, P], F32)
+        a_rows = [sbuf("a_rows%d" % i, [P, V], BF16) for i in range(TILES)]
+        r_rows = [sbuf("r_rows%d" % k, [P, R_BATCH, C], BF16) for k in range(TILES // R_BATCH)]
+        b_words = [sbuf("b_words%d" % n, [P, GROUPS, 2 * K_PASS], U8) for n in range(GROUPS)]
+        b_scales = sbuf("b_scales", [P, GROUPS, V], U8)
+        l_words = sbuf("l_words", [P, GROUPS, 2 * C], U8)
+        l_scales = sbuf("l_scales", [P, GROUPS, C], U8)
+        a_split = ring("a_split", [P, V], BF16)
+        a_turned = ring("a_turned", [P, V], BF16)
+        a_codes = ring("a_codes", [P, GROUPS * P], U32)
+        a_scales = ring("a_scales", [P, GROUPS * P], U8)
+        h_split = ring("h_split", [P, V], BF16)
+        h_turned = ring("h_turned", [P, V], BF16)
+        h_codes = ring("h_codes", [P, GROUPS * P], U32)
+        h_scales = ring("h_scales", [P, GROUPS * P], U8)
+        y_rows = ring("y_rows", [P, C], F32)
+        y_split = ring("y_split", [P, C], BF16)
+        y_turned = ring("y_turned", [P, C], BF16)
+        y_codes = sbuf("y_codes", [P, V], U32)
+        y_scales = sbuf("y_scales", [P, V], U8)
+
+        p_banks = [ps.tile([P, K_PASS], F32, name="p_bank%d" % n) for n in range(GROUPS)]
+        s_bank = ps.tile([P, C], F32, name="s_bank")
+        t_banks = [ps.tile([P, 4 * P], F32, name="t_bank%d" % k) for k in range(4)]
+
+        ctx.enter_context(tc.manual_schedule())
+
+        def natural(ap):
+            return ap.rearrange("p (m u e) -> p u m e", u=2, e=2)
+
+        def split(ap):
+            return ap.rearrange("p (u m e) -> p u m e", u=2, e=2)
+
+        def group(ap, g):
+            return ap[:, g * K_PASS : (g + 1) * K_PASS]
+
+        def load_a(i, cols):
+            nc.sync.dma_start(out=a_rows[i][:, cols], in_=adj[i * P : (i + 1) * P, cols])
+
+        def load_r(k):
+            rows = compat[k * R_BATCH * P : (k + 1) * R_BATCH * P, :]
+            nc.sync.dma_start(out=r_rows[k][:], in_=rows.rearrange("(s p) c -> p s c", p=P))
+
+        def load_scale_rows(plane, rows):
+            for q in range(4):
+                nc.sync.dma_start(
+                    out=plane[32 * q : 32 * q + 4, :, :].bitcast(I32),
+                    in_=rows[:, 4 * q : 4 * q + 4, :].rearrange("g r n -> r g n").bitcast(I32),
+                )
+
+        def load_words(tile, words):
+            nc.sync.dma_start(out=tile[:].bitcast(I32), in_=words.rearrange("g p b -> p g b").bitcast(I32))
+
+        def split_a(i):
+            nc.scalar.copy(
+                out=a_split[i % RING][:].bitcast(F32).rearrange("p (g u m) -> p g u m", g=GROUPS, u=2),
+                in_=a_rows[i][:].bitcast(F32).rearrange("p (g m u) -> p g u m", g=GROUPS, u=2),
+            )
+
+        def turn_split(src, g, bank, half):
+            words = group(src, g).bitcast(F32)
+            for u in range(2):
+                slot = 2 * half + u
+                nc.tensor.transpose(bank[:, slot * P : (slot + 1) * P], words[:, u * P : (u + 1) * P], ident[:])
+
+        def turn_natural(src, g, bank, half):
+            words = group(src, g).bitcast(F32)
+            for u in range(2):
+                slot = 2 * half + u
+                nc.tensor.transpose(bank[:, slot * P : (slot + 1) * P], words[:, u : 2 * P : 2], ident[:])
+
+        def interleave(dst, g, count, bank, half):
+            out = dst[:, g * K_PASS : (g + count) * K_PASS].bitcast(F32)
+            src = bank[:, half * 2 * P : (half + count) * 2 * P]
+            nc.scalar.copy(
+                out=out.rearrange("p (g r u) -> p g r u", g=count, u=2),
+                in_=src.rearrange("p (g u r) -> p g r u", g=count, u=2),
+            )
+
+        def quantize(codes, scales, turned, g, count):
+            cols = slice(g * P, (g + count) * P)
+            nc.vector.quantize_mx(
+                out=codes[:, cols].bitcast(FP8X4),
+                scales=scales[:, cols],
+                in_=turned[:, g * K_PASS : (g + count) * K_PASS],
+            )
+
+        def quantize_a(i, g, count):
+            quantize(a_codes[i % RING], a_scales[i % RING], a_turned[i % RING], g, count)
+
+        def quantize_h(i, g, count):
+            quantize(h_codes[i % RING], h_scales[i % RING], h_turned[i % RING], g, count)
+
+        def mx_pass(bank, codes, scales, g, words, word_scales):
+            cols = slice(g * P, (g + 1) * P)
+            nc.tensor.matmul_mx(
+                out=bank[:],
+                lhsT=codes[:, cols].bitcast(FP8X4),
+                lhsT_scale=scales[:, cols],
+                rhs=words.bitcast(FP4X4),
+                rhs_scale=word_scales,
+                start=(g == 0),
+                stop=(g == GROUPS - 1),
+            )
+
+        def paths(i, n):
+            for g in range(GROUPS):
+                mx_pass(
+                    p_banks[n], a_codes[i % RING], a_scales[i % RING], g,
+                    b_words[n][:, g, :], b_scales[:, g, n * K_PASS : (n + 1) * K_PASS],
+                )
+
+        def triangles(i, n):
+            nc.vector.tensor_tensor(
+                out=split(group(h_split[i % RING], n)),
+                in0=natural(p_banks[n][:]),
+                in1=natural(group(a_rows[i], n)),
+                op=MULT,
+            )
+
+        def scores(i):
+            for g in range(GROUPS):
+                mx_pass(s_bank, h_codes[i % RING], h_scales[i % RING], g, l_words[:, g, :], l_scales[:, g, :])
+
+        def epilogue(i, out, view):
+            nc.vector.scalar_tensor_tensor(
+                out=out,
+                in0=view(s_bank[:]),
+                scalar=HALF,
+                in1=view(r_rows[i // R_BATCH][:, i % R_BATCH, :]),
+                op0=MULT,
+                op1=MULT,
+            )
+
+        def result(i):
+            epilogue(i, y_rows[i % RING][:], lambda ap: ap)
+            nc.sync.dma_start(out=out_0[i * P : (i + 1) * P, :], in_=y_rows[i % RING][:])
+
+        def round_y(i):
+            nc.scalar.copy(out=split(y_split[i % RING][:]), in_=natural(y_rows[i % RING][:]))
+
+        def quantize_y(i):
+            cols = slice(i * P, (i + 1) * P)
+            nc.vector.quantize_mx(
+                out=y_codes[:, cols].bitcast(FP8X4), scales=y_scales[:, cols], in_=y_turned[i % RING][:]
+            )
+
+        def store_codes(first, last):
+            cols = slice(first * P, last * P)
+            words = out_1[0].rearrange("p m t -> p (m t)").bitcast(I32)
+            nc.sync.dma_start(out=words[:, cols], in_=y_codes[:, cols].bitcast(I32))
+
+        make_identity(nc, ident[:])
+        nc.vector.memset(b_scales[:].rearrange("p g n -> p (g n)").bitcast(U32), 0)
+        nc.vector.memset(l_scales[:].rearrange("p g n -> p (g n)").bitcast(U32), 0)
+        for g in range(GROUPS):
+            load_a(0, slice(g * K_PASS, (g + 1) * K_PASS))
+        load_a(1, slice(0, V))
+        load_scale_rows(b_scales, adj4_scales)
+        for n in range(GROUPS):
+            load_words(b_words[n], adj4_words[:, :, 2 * n * K_PASS : 2 * (n + 1) * K_PASS])
+        load_a(2, slice(0, V))
+        load_scale_rows(l_scales, lab_scales)
+        load_words(l_words, lab_words)
+        for i in range(3, TILES):
+            if i % R_BATCH == 3:
+                load_r(i // R_BATCH)
+            load_a(i, slice(0, V))
+
+        for g in range(GROUPS):
+            turn_natural(a_rows[0], g, t_banks[1 + g], 0)
+            interleave(a_turned[0], g, 1, t_banks[1 + g], 0)
+            quantize_a(0, g, 1)
+
+        last = TILES - 1
+        for s in range(TILES):
+            ia, ih, iy, it = s + 1, s - 1, s - 2, s - 3
+            if ia <= last:
+                for g in range(GROUPS):
+                    if ia == 1:
+                        turn_natural(a_rows[ia], g, t_banks[g // 2], g % 2)
+                    else:
+                        turn_split(a_split[ia % RING], g, t_banks[g // 2], g % 2)
+            if it >= 0:
+                turn_split(y_split[it % RING], 0, t_banks[1], 1)
+            if ih >= 0:
+                for g in range(GROUPS):
+                    turn_split(h_split[ih % RING], g, t_banks[2 + g // 2], g % 2)
+            if iy >= 0:
+                result(iy)
+            if ia <= last:
+                interleave(a_turned[ia % RING], 0, 2, t_banks[0], 0)
+                interleave(a_turned[ia % RING], 2, 1, t_banks[1], 0)
+            if ih >= 0:
+                interleave(h_turned[ih % RING], 0, 2, t_banks[2], 0)
+                interleave(h_turned[ih % RING], 2, 1, t_banks[3], 0)
+            if it >= 0:
+                interleave(y_turned[it % RING], 0, 1, t_banks[1], 1)
+            paths(s, 0)
+            if ia <= last:
+                quantize_a(ia, 0, 2)
+                quantize_a(ia, 2, 1)
+            triangles(s, 0)
+            paths(s, 1)
+            if ih >= 0:
+                quantize_h(ih, 0, 2)
+                quantize_h(ih, 2, 1)
+            triangles(s, 1)
+            if s == last:
+                break
+            paths(s, 2)
+            triangles(s, 2)
+            if ih >= 0:
+                scores(ih)
+            if it >= 0:
+                quantize_y(it)
+                if it % 4 == 3:
+                    store_codes(it - 3, it + 1)
+            if iy >= 0:
+                round_y(iy)
+            if s + 2 <= last:
+                split_a(s + 2)
+
+        round_y(last - 2)
+        scores(last - 1)
+        paths(last, 2)
+        quantize_y(last - 3)
+        result(last - 1)
+        round_y(last - 1)
+        triangles(last, 2)
+        turn_split(y_split[(last - 2) % RING], 0, t_banks[1], 0)
+        for g in range(GROUPS):
+            bank = t_banks[(2, 3, 0)[g]]
+            turn_split(h_split[last % RING], g, bank, 0)
+            interleave(h_turned[last % RING], g, 1, bank, 0)
+            quantize_h(last, g, 1)
+        turn_split(y_split[(last - 1) % RING], 0, t_banks[1], 1)
+        scores(last)
+        for k in range(2):
+            interleave(y_turned[(last - 2 + k) % RING], 0, 1, t_banks[1], k)
+            quantize_y(last - 2 + k)
+        store_codes(8, last)
+        for u in range(2):
+            epilogue(last, split(y_split[last % RING][:])[:, u], lambda ap: natural(ap)[:, u])
+        result(last)
+        turn_split(y_split[last % RING], 0, t_banks[2], 0)
+        interleave(y_turned[last % RING], 0, 1, t_banks[2], 0)
+        quantize_y(last)
+        store_codes(last, TILES)
+        rows = out_2[0].bitcast(I32)
+        for q in range(4):
+            queue = nc.sync if q % 2 == 0 else nc.scalar
+            queue.dma_start(out=rows[4 * q : 4 * q + 4, :], in_=y_scales[32 * q : 32 * q + 4, :].bitcast(I32))

@@ -19,7 +19,7 @@ P = 128
 K_PASS = 512
 GROUPS = V // K_PASS
 TILES = V // P
-RING = 3
+RING = 4
 R_BATCH = 4
 HALF = 0.5
 
@@ -35,33 +35,27 @@ def tile_triangle_label_scores_h1_kernel(
         def sbuf(name, shape, dtype):
             return sb.tile(shape, dtype, name=name, align_bytes=64)
 
-        def ring(name, shape, dtype):
-            return [sbuf("%s%d" % (name, k), shape, dtype) for k in range(RING)]
-
         ident = sbuf("ident", [P, P], F32)
         a_rows = [sbuf("a_rows%d" % i, [P, V], BF16) for i in range(TILES)]
         r_rows = [sbuf("r_rows%d" % k, [P, R_BATCH, C], BF16) for k in range(TILES // R_BATCH)]
-        b_words = [sbuf("b_words%d" % n, [P, GROUPS, 2 * K_PASS], U8) for n in range(GROUPS)]
+        b_words = [sbuf("b_words%d" % g, [P, 2 * V], U8) for g in range(GROUPS)]
         b_scales = sbuf("b_scales", [P, GROUPS, V], U8)
         l_words = sbuf("l_words", [P, GROUPS, 2 * C], U8)
         l_scales = sbuf("l_scales", [P, GROUPS, C], U8)
-        a_split = ring("a_split", [P, V], BF16)
-        a_turned = ring("a_turned", [P, V], BF16)
-        a_codes = ring("a_codes", [P, GROUPS * P], U32)
-        a_scales = ring("a_scales", [P, GROUPS * P], U8)
-        h_split = ring("h_split", [P, V], BF16)
-        h_turned = ring("h_turned", [P, V], BF16)
-        h_codes = ring("h_codes", [P, GROUPS * P], U32)
-        h_scales = ring("h_scales", [P, GROUPS * P], U8)
-        y_rows = ring("y_rows", [P, C], F32)
-        y_split = ring("y_split", [P, C], BF16)
-        y_turned = ring("y_turned", [P, C], BF16)
+        a_split = sbuf("a_split", [P, RING * V], BF16)
+        a_turned = sbuf("a_turned", [P, RING * V], BF16)
+        a_codes = sbuf("a_codes", [P, RING * GROUPS * P], U32)
+        a_scales = sbuf("a_scales", [P, RING * GROUPS * P], U8)
+        h_split = sbuf("h_split", [P, RING * V], BF16)
+        h_turned = sbuf("h_turned", [P, RING * V], BF16)
+        h_codes = sbuf("h_codes", [P, RING * GROUPS * P], U32)
+        h_scales = sbuf("h_scales", [P, RING * GROUPS * P], U8)
+        y_rows = sbuf("y_rows", [P, RING, C], F32)
+        y_split = sbuf("y_split", [P, TILES * C], BF16)
+        y_turned = sbuf("y_turned", [P, TILES * C], BF16)
         y_codes = sbuf("y_codes", [P, V], U32)
         y_scales = sbuf("y_scales", [P, V], U8)
-
-        p_banks = [ps.tile([P, K_PASS], F32, name="p_bank%d" % n) for n in range(GROUPS)]
-        s_bank = ps.tile([P, C], F32, name="s_bank")
-        t_banks = [ps.tile([P, 4 * P], F32, name="t_bank%d" % k) for k in range(4)]
+        bank = [ps.tile([P, K_PASS], F32, name="bank%d" % b) for b in range(8)]
 
         ctx.enter_context(tc.manual_schedule())
 
@@ -71,8 +65,14 @@ def tile_triangle_label_scores_h1_kernel(
         def split(ap):
             return ap.rearrange("p (u m e) -> p u m e", u=2, e=2)
 
-        def group(ap, g):
-            return ap[:, g * K_PASS : (g + 1) * K_PASS]
+        def span(ap, first, count):
+            return ap[:, first * K_PASS : (first + count) * K_PASS]
+
+        def a_at(i):
+            return (i + 1) % RING * GROUPS
+
+        def h_at(i):
+            return i % RING * GROUPS
 
         def load_a(i, cols):
             nc.sync.dma_start(out=a_rows[i][:, cols], in_=adj[i * P : (i + 1) * P, cols])
@@ -88,53 +88,46 @@ def tile_triangle_label_scores_h1_kernel(
                     in_=rows[:, 4 * q : 4 * q + 4, :].rearrange("g r n -> r g n").bitcast(I32),
                 )
 
-        def load_words(tile, words):
-            nc.sync.dma_start(out=tile[:].bitcast(I32), in_=words.rearrange("g p b -> p g b").bitcast(I32))
+        def load_b(g):
+            nc.sync.dma_start(out=b_words[g][:].bitcast(I32), in_=adj4_words[g].bitcast(I32))
 
-        def split_a(i):
-            nc.scalar.copy(
-                out=a_split[i % RING][:].bitcast(F32).rearrange("p (g u m) -> p g u m", g=GROUPS, u=2),
-                in_=a_rows[i][:].bitcast(F32).rearrange("p (g m u) -> p g u m", g=GROUPS, u=2),
+        def split_a(copy, i, g, count):
+            copy(
+                out=span(a_split, a_at(i) + g, count).bitcast(F32).rearrange("p (g u m) -> p g u m", g=count, u=2),
+                in_=span(a_rows[i], g, count).bitcast(F32).rearrange("p (g m u) -> p g u m", g=count, u=2),
             )
 
-        def turn_split(src, g, bank, half):
-            words = group(src, g).bitcast(F32)
-            for u in range(2):
-                slot = 2 * half + u
-                nc.tensor.transpose(bank[:, slot * P : (slot + 1) * P], words[:, u * P : (u + 1) * P], ident[:])
+        def turn(src, first, count, b):
+            words = span(src, first, count).bitcast(F32)
+            for k in range(2 * count):
+                cols = slice(k * P, (k + 1) * P)
+                nc.tensor.transpose(bank[b][:, cols], words[:, cols], ident[:])
 
-        def turn_natural(src, g, bank, half):
-            words = group(src, g).bitcast(F32)
-            for u in range(2):
-                slot = 2 * half + u
-                nc.tensor.transpose(bank[:, slot * P : (slot + 1) * P], words[:, u : 2 * P : 2], ident[:])
-
-        def interleave(dst, g, count, bank, half):
-            out = dst[:, g * K_PASS : (g + count) * K_PASS].bitcast(F32)
-            src = bank[:, half * 2 * P : (half + count) * 2 * P]
+        def interleave(dst, first, count, b):
             nc.scalar.copy(
-                out=out.rearrange("p (g r u) -> p g r u", g=count, u=2),
-                in_=src.rearrange("p (g u r) -> p g r u", g=count, u=2),
+                out=span(dst, first, count).bitcast(F32).rearrange("p (g r u) -> p g r u", g=count, u=2),
+                in_=bank[b][:, : count * 2 * P].rearrange("p (g u r) -> p g r u", g=count, u=2),
             )
 
-        def quantize(codes, scales, turned, g, count):
-            cols = slice(g * P, (g + count) * P)
+        def quantize(codes, scales, turned, first, count):
+            cols = slice(first * P, (first + count) * P)
             nc.vector.quantize_mx(
-                out=codes[:, cols].bitcast(FP8X4),
-                scales=scales[:, cols],
-                in_=turned[:, g * K_PASS : (g + count) * K_PASS],
+                out=codes[:, cols].bitcast(FP8X4), scales=scales[:, cols], in_=span(turned, first, count)
             )
 
-        def quantize_a(i, g, count):
-            quantize(a_codes[i % RING], a_scales[i % RING], a_turned[i % RING], g, count)
+        def quantize_a(first, count):
+            quantize(a_codes, a_scales, a_turned, first, count)
 
-        def quantize_h(i, g, count):
-            quantize(h_codes[i % RING], h_scales[i % RING], h_turned[i % RING], g, count)
+        def quantize_h(first, count):
+            quantize(h_codes, h_scales, h_turned, first, count)
 
-        def mx_pass(bank, codes, scales, g, words, word_scales):
-            cols = slice(g * P, (g + 1) * P)
+        def quantize_y(first, count):
+            quantize(y_codes, y_scales, y_turned, first, count)
+
+        def mx_pass(b, codes, scales, at, g, words, word_scales):
+            cols = slice((at + g) * P, (at + g + 1) * P)
             nc.tensor.matmul_mx(
-                out=bank[:],
+                out=bank[b][:],
                 lhsT=codes[:, cols].bitcast(FP8X4),
                 lhsT_scale=scales[:, cols],
                 rhs=words.bitcast(FP4X4),
@@ -143,150 +136,192 @@ def tile_triangle_label_scores_h1_kernel(
                 stop=(g == GROUPS - 1),
             )
 
-        def paths(i, n):
-            for g in range(GROUPS):
-                mx_pass(
-                    p_banks[n], a_codes[i % RING], a_scales[i % RING], g,
-                    b_words[n][:, g, :], b_scales[:, g, n * K_PASS : (n + 1) * K_PASS],
-                )
+        def path_pass(i, n, g, b):
+            words = b_words[g][:, 2 * n * K_PASS : 2 * (n + 1) * K_PASS]
+            mx_pass(b, a_codes, a_scales, a_at(i), g, words, span(b_scales[:, g, :], n, 1))
 
-        def triangles(i, n):
+        def paths(i, n, b):
+            for g in range(GROUPS):
+                path_pass(i, n, g, b)
+
+        def triangles(i, n, b):
             nc.vector.tensor_tensor(
-                out=split(group(h_split[i % RING], n)),
-                in0=natural(p_banks[n][:]),
-                in1=natural(group(a_rows[i], n)),
+                out=split(span(h_split, h_at(i) + n, 1)),
+                in0=natural(bank[b][:]),
+                in1=natural(span(a_rows[i], n, 1)),
                 op=MULT,
             )
 
-        def scores(i):
+        def scores(i, b):
             for g in range(GROUPS):
-                mx_pass(s_bank, h_codes[i % RING], h_scales[i % RING], g, l_words[:, g, :], l_scales[:, g, :])
+                mx_pass(b, h_codes, h_scales, h_at(i), g, l_words[:, g, :], l_scales[:, g, :])
 
-        def epilogue(i, out, view):
-            nc.vector.scalar_tensor_tensor(
-                out=out,
-                in0=view(s_bank[:]),
-                scalar=HALF,
-                in1=view(r_rows[i // R_BATCH][:, i % R_BATCH, :]),
-                op0=MULT,
-                op1=MULT,
-            )
+        def epilogue(out, sums, factors):
+            nc.vector.scalar_tensor_tensor(out=out, in0=sums, scalar=HALF, in1=factors, op0=MULT, op1=MULT)
 
-        def result(i):
-            epilogue(i, y_rows[i % RING][:], lambda ap: ap)
-            nc.sync.dma_start(out=out_0[i * P : (i + 1) * P, :], in_=y_rows[i % RING][:])
+        def compat_rows(i):
+            return r_rows[i // R_BATCH][:, i % R_BATCH, :]
+
+        def result(i, b):
+            epilogue(y_rows[:, i % RING, :], bank[b][:], compat_rows(i))
+            nc.sync.dma_start(out=out_0[i * P : (i + 1) * P, :], in_=y_rows[:, i % RING, :])
 
         def round_y(i):
-            nc.scalar.copy(out=split(y_split[i % RING][:]), in_=natural(y_rows[i % RING][:]))
+            nc.scalar.copy(out=split(span(y_split, i, 1)), in_=natural(y_rows[:, i % RING, :]))
 
-        def quantize_y(i):
-            cols = slice(i * P, (i + 1) * P)
-            nc.vector.quantize_mx(
-                out=y_codes[:, cols].bitcast(FP8X4), scales=y_scales[:, cols], in_=y_turned[i % RING][:]
-            )
-
-        def store_codes(first, last):
-            cols = slice(first * P, last * P)
+        def store_codes(first, count):
+            cols = slice(first * P, (first + count) * P)
             words = out_1[0].rearrange("p m t -> p (m t)").bitcast(I32)
             nc.sync.dma_start(out=words[:, cols], in_=y_codes[:, cols].bitcast(I32))
+
+        def warm_up(count):
+            for k in range(count):
+                nc.tensor.transpose(bank[4][:, (k % 4) * P : (k % 4 + 1) * P], ident[:], ident[:])
 
         make_identity(nc, ident[:])
         nc.vector.memset(b_scales[:].rearrange("p g n -> p (g n)").bitcast(U32), 0)
         nc.vector.memset(l_scales[:].rearrange("p g n -> p (g n)").bitcast(U32), 0)
         for g in range(GROUPS):
             load_a(0, slice(g * K_PASS, (g + 1) * K_PASS))
-        load_a(1, slice(0, V))
         load_scale_rows(b_scales, adj4_scales)
-        for n in range(GROUPS):
-            load_words(b_words[n], adj4_words[:, :, 2 * n * K_PASS : 2 * (n + 1) * K_PASS])
-        load_a(2, slice(0, V))
+        load_b(0)
+        load_a(1, slice(0, V))
+        load_b(1)
+        load_b(2)
+        for i in range(2, 5):
+            load_a(i, slice(0, V))
         load_scale_rows(l_scales, lab_scales)
-        load_words(l_words, lab_words)
-        for i in range(3, TILES):
+        nc.sync.dma_start(out=l_words[:].bitcast(I32), in_=lab_words.rearrange("g p b -> p g b").bitcast(I32))
+        load_r(0)
+        for i in range(5, TILES):
+            load_a(i, slice(0, V))
             if i % R_BATCH == 3:
                 load_r(i // R_BATCH)
-            load_a(i, slice(0, V))
 
+        warm_up(8)
         for g in range(GROUPS):
-            turn_natural(a_rows[0], g, t_banks[1 + g], 0)
-            interleave(a_turned[0], g, 1, t_banks[1 + g], 0)
-            quantize_a(0, g, 1)
+            split_a(nc.vector.tensor_copy, 0, g, 1)
+        for g in range(GROUPS):
+            turn(a_split, a_at(0) + g, 1, g)
+            interleave(a_turned, a_at(0) + g, 1, g)
+            quantize_a(a_at(0) + g, 1)
+        warm_up(8)
+        split_a(nc.vector.tensor_copy, 1, 0, GROUPS)
+        for g in range(GROUPS):
+            for n in range(GROUPS):
+                path_pass(0, n, g, 7 - n)
+            if g == 0:
+                for first, count, b in ((0, 2, 3), (2, 1, 4)):
+                    turn(a_split, a_at(1) + first, count, b)
+                    interleave(a_turned, a_at(1) + first, count, b)
+                    quantize_a(a_at(1) + first, count)
+        split_a(nc.scalar.copy, 2, 0, GROUPS)
+        for n in range(GROUPS):
+            triangles(0, n, 7 - n)
+        for n in range(2):
+            paths(1, n, n)
+            triangles(1, n, n)
+        for first, count, b in ((0, 2, 3), (2, 1, 4)):
+            turn(a_split, a_at(2) + first, count, b)
+        split_a(nc.scalar.copy, 3, 0, GROUPS)
+        for first, count, b in ((0, 2, 3), (2, 1, 4)):
+            interleave(a_turned, a_at(2) + first, count, b)
+            quantize_a(a_at(2) + first, count)
+        split_a(nc.scalar.copy, 4, 0, GROUPS)
+        paths(1, 2, 2)
+        triangles(1, 2, 2)
 
         last = TILES - 1
-        for s in range(TILES):
-            ia, ih, iy, it = s + 1, s - 1, s - 2, s - 3
-            if ia <= last:
-                for g in range(GROUPS):
-                    if ia == 1:
-                        turn_natural(a_rows[ia], g, t_banks[g // 2], g % 2)
-                    else:
-                        turn_split(a_split[ia % RING], g, t_banks[g // 2], g % 2)
-            if it >= 0:
-                turn_split(y_split[it % RING], 0, t_banks[1], 1)
-            if ih >= 0:
-                for g in range(GROUPS):
-                    turn_split(h_split[ih % RING], g, t_banks[2 + g // 2], g % 2)
-            if iy >= 0:
-                result(iy)
-            if ia <= last:
-                interleave(a_turned[ia % RING], 0, 2, t_banks[0], 0)
-                interleave(a_turned[ia % RING], 2, 1, t_banks[1], 0)
-            if ih >= 0:
-                interleave(h_turned[ih % RING], 0, 2, t_banks[2], 0)
-                interleave(h_turned[ih % RING], 2, 1, t_banks[3], 0)
-            if it >= 0:
-                interleave(y_turned[it % RING], 0, 1, t_banks[1], 1)
-            paths(s, 0)
-            if ia <= last:
-                quantize_a(ia, 0, 2)
-                quantize_a(ia, 2, 1)
-            triangles(s, 0)
-            paths(s, 1)
-            if ih >= 0:
-                quantize_h(ih, 0, 2)
-                quantize_h(ih, 2, 1)
-            triangles(s, 1)
-            if s == last:
+        for a in range(2, TILES, 2):
+            b = a + 1
+            a_units = [(a_at(b) + 2 * k, 2, k) for k in range(3)] if b < last else [(a_at(b), 2, 0), (a_at(b) + 2, 1, 1)]
+            h_units = [(h_at(a - 2) + 2 * k, 2, 3 + k) for k in range(3)]
+            for first, count, k in a_units:
+                turn(a_split, first, count, k)
+            for first, count, k in h_units:
+                turn(h_split, first, count, k)
+            if a >= 6:
+                turn(y_split, a - 6, 2, 6)
+            for first, count, k in a_units:
+                interleave(a_turned, first, count, k)
+                quantize_a(first, count)
+            for first, count, k in h_units:
+                interleave(h_turned, first, count, k)
+            if a >= 6:
+                interleave(y_turned, a - 6, 2, 6)
+            paths(a, 0, 7)
+            quantize_h(h_units[0][0], 2)
+            quantize_h(h_units[1][0], 2)
+            triangles(a, 0, 7)
+            paths(a, 1, 0)
+            quantize_h(h_units[2][0], 2)
+            triangles(a, 1, 0)
+            paths(a, 2, 1)
+            triangles(a, 2, 1)
+            if a >= 6:
+                quantize_y(a - 6, 2)
+            if a == 8:
+                store_codes(0, 4)
+            if a >= 4:
+                round_y(a - 4)
+                round_y(b - 4)
+            if b == last:
                 break
-            paths(s, 2)
-            triangles(s, 2)
-            if ih >= 0:
-                scores(ih)
-            if it >= 0:
-                quantize_y(it)
-                if it % 4 == 3:
-                    store_codes(it - 3, it + 1)
-            if iy >= 0:
-                round_y(iy)
-            if s + 2 <= last:
-                split_a(s + 2)
+            for i in (b + 2, b + 3):
+                if i <= last:
+                    split_a(nc.scalar.copy, i, 0, GROUPS)
+            for n in range(GROUPS):
+                paths(b, n, 2 + n)
+                triangles(b, n, 2 + n)
+            scores(a - 2, 5)
+            result(a - 2, 5)
+            scores(b - 2, 6)
+            result(b - 2, 6)
 
+        scores(last - 3, 2)
+        result(last - 3, 2)
+        scores(last - 2, 3)
+        result(last - 2, 3)
+        h_units = [(h_at(last - 1), 2, 4), (h_at(last - 1) + 2, 1, 5)]
+        for first, count, k in h_units:
+            turn(h_split, first, count, k)
+        turn(y_split, last - 5, 2, 6)
+        for first, count, k in h_units:
+            interleave(h_turned, first, count, k)
+            quantize_h(first, count)
+        interleave(y_turned, last - 5, 2, 6)
+        round_y(last - 3)
         round_y(last - 2)
-        scores(last - 1)
-        paths(last, 2)
-        quantize_y(last - 3)
-        result(last - 1)
+        paths(last, 0, 7)
+        triangles(last, 0, 7)
+        quantize_y(last - 5, 2)
+        store_codes(4, 4)
+        paths(last, 1, 0)
+        triangles(last, 1, 0)
+        scores(last - 1, 1)
+        result(last - 1, 1)
         round_y(last - 1)
-        triangles(last, 2)
-        turn_split(y_split[(last - 2) % RING], 0, t_banks[1], 0)
-        for g in range(GROUPS):
-            bank = t_banks[(2, 3, 0)[g]]
-            turn_split(h_split[last % RING], g, bank, 0)
-            interleave(h_turned[last % RING], g, 1, bank, 0)
-            quantize_h(last, g, 1)
-        turn_split(y_split[(last - 1) % RING], 0, t_banks[1], 1)
-        scores(last)
-        for k in range(2):
-            interleave(y_turned[(last - 2 + k) % RING], 0, 1, t_banks[1], k)
-            quantize_y(last - 2 + k)
-        store_codes(8, last)
+        paths(last, 2, 2)
+        triangles(last, 2, 2)
+        turn(y_split, last - 3, 2, 6)
+        for g, k in enumerate((4, 5, 3)):
+            turn(h_split, h_at(last) + g, 1, k)
+            interleave(h_turned, h_at(last) + g, 1, k)
+            quantize_h(h_at(last) + g, 1)
+        turn(y_split, last - 1, 1, 7)
+        scores(last, 0)
+        interleave(y_turned, last - 3, 2, 6)
+        quantize_y(last - 3, 2)
+        interleave(y_turned, last - 1, 1, 7)
+        quantize_y(last - 1, 1)
+        store_codes(8, 3)
         for u in range(2):
-            epilogue(last, split(y_split[last % RING][:])[:, u], lambda ap: natural(ap)[:, u])
-        result(last)
-        turn_split(y_split[last % RING], 0, t_banks[2], 0)
-        interleave(y_turned[last % RING], 0, 1, t_banks[2], 0)
-        quantize_y(last)
-        store_codes(last, TILES)
+            epilogue(split(span(y_split, last, 1))[:, u], natural(bank[0][:])[:, u], natural(compat_rows(last))[:, u])
+        result(last, 0)
+        turn(y_split, last, 1, 1)
+        interleave(y_turned, last, 1, 1)
+        quantize_y(last, 1)
+        store_codes(last, 1)
         rows = out_2[0].bitcast(I32)
         for q in range(4):
             queue = nc.sync if q % 2 == 0 else nc.scalar

@@ -19,7 +19,7 @@ P = 128
 K_PASS = 512
 GROUPS = V // K_PASS
 TILES = V // P
-RING = 4
+RING = 6
 R_BATCH = 4
 HALF = 0.5
 
@@ -56,6 +56,11 @@ def tile_triangle_label_scores_h1_kernel(
         y_codes = sbuf("y_codes", [P, V], U32)
         y_scales = sbuf("y_scales", [P, V], U8)
         bank = [ps.tile([P, K_PASS], F32, name="bank%d" % b) for b in range(8)]
+        taken = []
+
+        def take():
+            taken.append(len(taken) % 8)
+            return taken[-1]
 
         ctx.enter_context(tc.manual_schedule())
 
@@ -72,7 +77,7 @@ def tile_triangle_label_scores_h1_kernel(
             return (i + 1) % RING * GROUPS
 
         def h_at(i):
-            return i % RING * GROUPS
+            return (i + 1) % RING * GROUPS
 
         def load_a(i, cols):
             nc.sync.dma_start(out=a_rows[i][:, cols], in_=adj[i * P : (i + 1) * P, cols])
@@ -103,8 +108,8 @@ def tile_triangle_label_scores_h1_kernel(
                 cols = slice(k * P, (k + 1) * P)
                 nc.tensor.transpose(bank[b][:, cols], words[:, cols], ident[:])
 
-        def interleave(dst, first, count, b):
-            nc.scalar.copy(
+        def interleave(copy, dst, first, count, b):
+            copy(
                 out=span(dst, first, count).bitcast(F32).rearrange("p (g r u) -> p g r u", g=count, u=2),
                 in_=bank[b][:, : count * 2 * P].rearrange("p (g u r) -> p g r u", g=count, u=2),
             )
@@ -174,20 +179,26 @@ def tile_triangle_label_scores_h1_kernel(
             words = out_1[0].rearrange("p m t -> p (m t)").bitcast(I32)
             nc.sync.dma_start(out=words[:, cols], in_=y_codes[:, cols].bitcast(I32))
 
+        def store_scales(first, count, queues):
+            cols = slice(first * P // 4, (first + count) * P // 4)
+            rows = out_2[0].bitcast(I32)
+            for q in range(4):
+                live = y_scales[32 * q : 32 * q + 4, :].bitcast(I32)
+                queues[q % 2].dma_start(out=rows[4 * q : 4 * q + 4, cols], in_=live[:, cols])
+
         def warm_up(count):
             for k in range(count):
-                nc.tensor.transpose(bank[4][:, (k % 4) * P : (k % 4 + 1) * P], ident[:], ident[:])
+                nc.tensor.transpose(bank[7][:, (k % 4) * P : (k % 4 + 1) * P], ident[:], ident[:])
 
         make_identity(nc, ident[:])
         nc.vector.memset(b_scales[:].rearrange("p g n -> p (g n)").bitcast(U32), 0)
         nc.vector.memset(l_scales[:].rearrange("p g n -> p (g n)").bitcast(U32), 0)
         for g in range(GROUPS):
             load_a(0, slice(g * K_PASS, (g + 1) * K_PASS))
-        load_scale_rows(b_scales, adj4_scales)
-        load_b(0)
         load_a(1, slice(0, V))
-        load_b(1)
-        load_b(2)
+        load_scale_rows(b_scales, adj4_scales)
+        for g in range(GROUPS):
+            load_b(g)
         for i in range(2, 5):
             load_a(i, slice(0, V))
         load_scale_rows(l_scales, lab_scales)
@@ -198,131 +209,126 @@ def tile_triangle_label_scores_h1_kernel(
             if i % R_BATCH == 3:
                 load_r(i // R_BATCH)
 
-        warm_up(8)
+        def units(first, count):
+            odd = [(first, 1)] if count % 2 else []
+            return odd + [(k, 2) for k in range(first + count % 2, first + count, 2)]
+
+        def move(src, dst, first, count, copy=nc.scalar.copy):
+            b = take()
+            turn(src, first, count, b)
+            interleave(copy, dst, first, count, b)
+
+        def stage_one(i, n):
+            b = take()
+            paths(i, n, b)
+            triangles(i, n, b)
+
+        def stage_two(i):
+            b = take()
+            scores(i, b)
+            result(i, b)
+
+        warm_up(4)
         for g in range(GROUPS):
             split_a(nc.vector.tensor_copy, 0, g, 1)
-        for g in range(GROUPS):
-            turn(a_split, a_at(0) + g, 1, g)
-            interleave(a_turned, a_at(0) + g, 1, g)
-            quantize_a(a_at(0) + g, 1)
-        warm_up(8)
         split_a(nc.vector.tensor_copy, 1, 0, GROUPS)
         for g in range(GROUPS):
+            move(a_split, a_turned, a_at(0) + g, 1)
+            quantize_a(a_at(0) + g, 1)
+        for unit in units(a_at(1), GROUPS):
+            move(a_split, a_turned, *unit)
+            quantize_a(*unit)
+        warm_up(8)
+        first_banks = [take() for n in range(GROUPS)]
+        for g in range(GROUPS):
             for n in range(GROUPS):
-                path_pass(0, n, g, 7 - n)
-            if g == 0:
-                for first, count, b in ((0, 2, 3), (2, 1, 4)):
-                    turn(a_split, a_at(1) + first, count, b)
-                    interleave(a_turned, a_at(1) + first, count, b)
-                    quantize_a(a_at(1) + first, count)
+                path_pass(0, n, g, first_banks[n])
         split_a(nc.scalar.copy, 2, 0, GROUPS)
         for n in range(GROUPS):
-            triangles(0, n, 7 - n)
-        for n in range(2):
-            paths(1, n, n)
-            triangles(1, n, n)
-        for first, count, b in ((0, 2, 3), (2, 1, 4)):
-            turn(a_split, a_at(2) + first, count, b)
+            triangles(0, n, first_banks[n])
         split_a(nc.scalar.copy, 3, 0, GROUPS)
-        for first, count, b in ((0, 2, 3), (2, 1, 4)):
-            interleave(a_turned, a_at(2) + first, count, b)
-            quantize_a(a_at(2) + first, count)
         split_a(nc.scalar.copy, 4, 0, GROUPS)
-        paths(1, 2, 2)
-        triangles(1, 2, 2)
+        for n in range(GROUPS):
+            stage_one(1, n)
 
         last = TILES - 1
-        for a in range(2, TILES, 2):
-            b = a + 1
-            a_units = [(a_at(b) + 2 * k, 2, k) for k in range(3)] if b < last else [(a_at(b), 2, 0), (a_at(b) + 2, 1, 1)]
-            h_units = [(h_at(a - 2) + 2 * k, 2, 3 + k) for k in range(3)]
-            for first, count, k in a_units:
-                turn(a_split, first, count, k)
-            for first, count, k in h_units:
-                turn(h_split, first, count, k)
-            if a >= 6:
-                turn(y_split, a - 6, 2, 6)
-            for first, count, k in a_units:
-                interleave(a_turned, first, count, k)
-                quantize_a(first, count)
-            for first, count, k in h_units:
-                interleave(h_turned, first, count, k)
-            if a >= 6:
-                interleave(y_turned, a - 6, 2, 6)
-            paths(a, 0, 7)
-            quantize_h(h_units[0][0], 2)
-            quantize_h(h_units[1][0], 2)
-            triangles(a, 0, 7)
-            paths(a, 1, 0)
-            quantize_h(h_units[2][0], 2)
-            triangles(a, 1, 0)
-            paths(a, 2, 1)
-            triangles(a, 2, 1)
-            if a >= 6:
-                quantize_y(a - 6, 2)
-            if a == 8:
-                store_codes(0, 4)
-            if a >= 4:
+        for a in range(2, last, 3):
+            a_units = units(a_at(a), 3 * GROUPS)
+            h_tiles = range(max(a - 3, 0), a)
+            h_units = units(h_at(h_tiles[0]), GROUPS * len(h_tiles))
+            y_tiles = range(max(a - 7, 0), max(a - 4, 0))
+            y_units = units(y_tiles.start, len(y_tiles))
+            for unit in a_units[:2]:
+                move(a_split, a_turned, *unit)
+            move(a_split, a_turned, *a_units[2], copy=nc.vector.tensor_copy)
+            for unit in a_units[:3]:
+                quantize_a(*unit)
+            for unit in h_units:
+                move(h_split, h_turned, *unit)
+            for unit in a_units[3:]:
+                move(a_split, a_turned, *unit)
+            for unit in y_units:
+                move(y_split, y_turned, *unit)
+            for i in range(a + 3, min(a + 6, TILES)):
+                split_a(nc.scalar.copy, i, 0, GROUPS)
+            if a > 2:
                 round_y(a - 4)
-                round_y(b - 4)
-            if b == last:
-                break
-            for i in (b + 2, b + 3):
-                if i <= last:
-                    split_a(nc.scalar.copy, i, 0, GROUPS)
-            for n in range(GROUPS):
-                paths(b, n, 2 + n)
-                triangles(b, n, 2 + n)
-            scores(a - 2, 5)
-            result(a - 2, 5)
-            scores(b - 2, 6)
-            result(b - 2, 6)
+            waiting = [(quantize_h, h_units[0])] + [(quantize_a, unit) for unit in a_units[3:]]
+            waiting = waiting + [(quantize_h, unit) for unit in h_units[1:]] + [(quantize_y, unit) for unit in y_units]
+            for k in range(3 * GROUPS):
+                b = take()
+                paths(a + k // GROUPS, k % GROUPS, b)
+                for job, unit in waiting[k : k + 1]:
+                    job(*unit)
+                triangles(a + k // GROUPS, k % GROUPS, b)
+            for i in h_tiles:
+                stage_two(i)
+                if i < h_tiles[-1]:
+                    round_y(i)
 
-        scores(last - 3, 2)
-        result(last - 3, 2)
-        scores(last - 2, 3)
-        result(last - 2, 3)
-        h_units = [(h_at(last - 1), 2, 4), (h_at(last - 1) + 2, 1, 5)]
-        for first, count, k in h_units:
-            turn(h_split, first, count, k)
-        turn(y_split, last - 5, 2, 6)
-        for first, count, k in h_units:
-            interleave(h_turned, first, count, k)
-            quantize_h(first, count)
-        interleave(y_turned, last - 5, 2, 6)
+        h_units = units(h_at(last - 3), 3 * GROUPS)
+        y_units = units(last - 7, 3)
+        store_codes(0, 4)
+        for unit in units(a_at(last), GROUPS):
+            move(a_split, a_turned, *unit)
+            quantize_a(*unit)
+        move(h_split, h_turned, *h_units[0])
+        move(h_split, h_turned, *h_units[1], copy=nc.vector.tensor_copy)
+        for unit in h_units[2:]:
+            move(h_split, h_turned, *unit)
+        for unit in y_units:
+            move(y_split, y_turned, *unit)
+        round_y(last - 4)
+        quantize_h(*h_units[0])
+        quantize_h(*h_units[1])
+        for n in range(GROUPS):
+            stage_one(last, n)
+            quantize_h(*h_units[2 + n])
+        stage_two(last - 3)
+        for unit in y_units:
+            quantize_y(*unit)
+        for unit in units(h_at(last), GROUPS):
+            move(h_split, h_turned, *unit)
+            quantize_h(*unit)
+        move(y_split, y_turned, last - 4, 1)
+        quantize_y(last - 4, 1)
         round_y(last - 3)
-        round_y(last - 2)
-        paths(last, 0, 7)
-        triangles(last, 0, 7)
-        quantize_y(last - 5, 2)
         store_codes(4, 4)
-        paths(last, 1, 0)
-        triangles(last, 1, 0)
-        scores(last - 1, 1)
-        result(last - 1, 1)
+        store_scales(0, 8, (nc.sync, nc.sync))
+        stage_two(last - 2)
+        round_y(last - 2)
+        stage_two(last - 1)
         round_y(last - 1)
-        paths(last, 2, 2)
-        triangles(last, 2, 2)
-        turn(y_split, last - 3, 2, 6)
-        for g, k in enumerate((4, 5, 3)):
-            turn(h_split, h_at(last) + g, 1, k)
-            interleave(h_turned, h_at(last) + g, 1, k)
-            quantize_h(h_at(last) + g, 1)
-        turn(y_split, last - 1, 1, 7)
-        scores(last, 0)
-        interleave(y_turned, last - 3, 2, 6)
-        quantize_y(last - 3, 2)
-        interleave(y_turned, last - 1, 1, 7)
-        quantize_y(last - 1, 1)
-        store_codes(8, 3)
+        b = take()
+        scores(last, b)
         for u in range(2):
-            epilogue(split(span(y_split, last, 1))[:, u], natural(bank[0][:])[:, u], natural(compat_rows(last))[:, u])
-        result(last, 0)
-        turn(y_split, last, 1, 1)
-        interleave(y_turned, last, 1, 1)
-        quantize_y(last, 1)
-        store_codes(last, 1)
-        rows = out_2[0].bitcast(I32)
-        for q in range(4):
-            queue = nc.sync if q % 2 == 0 else nc.scalar
-            queue.dma_start(out=rows[4 * q : 4 * q + 4, :], in_=y_scales[32 * q : 32 * q + 4, :].bitcast(I32))
+            epilogue(split(span(y_split, last, 1))[:, u], natural(bank[b][:])[:, u], natural(compat_rows(last))[:, u])
+        result(last, b)
+        move(y_split, y_turned, last - 3, 2)
+        quantize_y(last - 3, 2)
+        store_codes(last - 3, 2)
+        move(y_split, y_turned, last - 1, 1)
+        move(y_split, y_turned, last, 1)
+        quantize_y(last - 1, 2)
+        store_codes(last - 1, 2)
+        store_scales(8, 4, (nc.sync, nc.scalar))

@@ -19,7 +19,7 @@ P = 128
 K_PASS = 512
 GROUPS = V // K_PASS
 TILES = V // P
-RING = 6
+RING = 4
 R_BATCH = 4
 HALF = 0.5
 
@@ -77,7 +77,7 @@ def tile_triangle_label_scores_h1_kernel(
             return (i + 1) % RING * GROUPS
 
         def h_at(i):
-            return (i + 1) % RING * GROUPS
+            return i % RING * GROUPS
 
         def load_a(i, cols):
             nc.sync.dma_start(out=a_rows[i][:, cols], in_=adj[i * P : (i + 1) * P, cols])
@@ -193,8 +193,7 @@ def tile_triangle_label_scores_h1_kernel(
         make_identity(nc, ident[:])
         nc.vector.memset(b_scales[:].rearrange("p g n -> p (g n)").bitcast(U32), 0)
         nc.vector.memset(l_scales[:].rearrange("p g n -> p (g n)").bitcast(U32), 0)
-        for g in range(GROUPS):
-            load_a(0, slice(g * K_PASS, (g + 1) * K_PASS))
+        load_a(0, slice(0, V))
         load_a(1, slice(0, V))
         load_scale_rows(b_scales, adj4_scales)
         for g in range(GROUPS):
@@ -228,14 +227,10 @@ def tile_triangle_label_scores_h1_kernel(
             scores(i, b)
             result(i, b)
 
-        warm_up(4)
-        for g in range(GROUPS):
-            split_a(nc.vector.tensor_copy, 0, g, 1)
+        warm_up(8)
+        split_a(nc.vector.tensor_copy, 0, 0, GROUPS)
         split_a(nc.vector.tensor_copy, 1, 0, GROUPS)
-        for g in range(GROUPS):
-            move(a_split, a_turned, a_at(0) + g, 1)
-            quantize_a(a_at(0) + g, 1)
-        for unit in units(a_at(1), GROUPS):
+        for unit in units(a_at(0), 2 * GROUPS):
             move(a_split, a_turned, *unit)
             quantize_a(*unit)
         warm_up(8)
@@ -252,83 +247,57 @@ def tile_triangle_label_scores_h1_kernel(
             stage_one(1, n)
 
         last = TILES - 1
-        for a in range(2, last, 3):
-            a_units = units(a_at(a), 3 * GROUPS)
-            h_tiles = range(max(a - 3, 0), a)
-            h_units = units(h_at(h_tiles[0]), GROUPS * len(h_tiles))
-            y_tiles = range(max(a - 7, 0), max(a - 4, 0))
-            y_units = units(y_tiles.start, len(y_tiles))
-            for unit in a_units[:2]:
+        for a in range(2, TILES, 2):
+            b = a + 1
+            a_units = units(a_at(b), GROUPS * (2 if b < last else 1))
+            if a == 2:
+                a_units = units(a_at(a), GROUPS) + a_units
+            h_units = units(h_at(a - 2), 2 * GROUPS)
+            for unit in a_units:
                 move(a_split, a_turned, *unit)
-            move(a_split, a_turned, *a_units[2], copy=nc.vector.tensor_copy)
-            for unit in a_units[:3]:
                 quantize_a(*unit)
             for unit in h_units:
                 move(h_split, h_turned, *unit)
-            for unit in a_units[3:]:
-                move(a_split, a_turned, *unit)
-            for unit in y_units:
-                move(y_split, y_turned, *unit)
-            for i in range(a + 3, min(a + 6, TILES)):
+            if a >= 6:
+                move(y_split, y_turned, a - 6, 2)
+            for i in range(b + 2, min(b + 4, TILES)):
                 split_a(nc.scalar.copy, i, 0, GROUPS)
-            if a > 2:
+            if a >= 4:
                 round_y(a - 4)
-            waiting = [(quantize_h, h_units[0])] + [(quantize_a, unit) for unit in a_units[3:]]
-            waiting = waiting + [(quantize_h, unit) for unit in h_units[1:]] + [(quantize_y, unit) for unit in y_units]
-            for k in range(3 * GROUPS):
-                b = take()
-                paths(a + k // GROUPS, k % GROUPS, b)
+                round_y(b - 4)
+            waiting = [(quantize_h, unit) for unit in h_units]
+            if a >= 6:
+                waiting = waiting + [(quantize_y, (a - 6, 2))]
+            for k in range(2 * GROUPS):
+                bk = take()
+                paths(a + k // GROUPS, k % GROUPS, bk)
                 for job, unit in waiting[k : k + 1]:
                     job(*unit)
-                triangles(a + k // GROUPS, k % GROUPS, b)
-            for i in h_tiles:
-                stage_two(i)
-                if i < h_tiles[-1]:
-                    round_y(i)
+                triangles(a + k // GROUPS, k % GROUPS, bk)
+            if a >= 6:
+                store_codes(a - 6, 2)
+            stage_two(a - 2)
+            if b < last:
+                stage_two(b - 2)
 
-        h_units = units(h_at(last - 3), 3 * GROUPS)
-        y_units = units(last - 7, 3)
-        store_codes(0, 4)
-        for unit in units(a_at(last), GROUPS):
-            move(a_split, a_turned, *unit)
-            quantize_a(*unit)
-        move(h_split, h_turned, *h_units[0])
-        move(h_split, h_turned, *h_units[1], copy=nc.vector.tensor_copy)
-        for unit in h_units[2:]:
-            move(h_split, h_turned, *unit)
-        for unit in y_units:
-            move(y_split, y_turned, *unit)
-        round_y(last - 4)
-        quantize_h(*h_units[0])
-        quantize_h(*h_units[1])
-        for n in range(GROUPS):
-            stage_one(last, n)
-            quantize_h(*h_units[2 + n])
-        stage_two(last - 3)
-        for unit in y_units:
-            quantize_y(*unit)
-        for unit in units(h_at(last), GROUPS):
+        store_scales(0, 6, (nc.sync, nc.sync))
+        for unit in units(h_at(last - 1), 2 * GROUPS):
             move(h_split, h_turned, *unit)
             quantize_h(*unit)
-        move(y_split, y_turned, last - 4, 1)
-        quantize_y(last - 4, 1)
+        move(y_split, y_turned, last - 5, 2)
         round_y(last - 3)
-        store_codes(4, 4)
-        store_scales(0, 8, (nc.sync, nc.sync))
-        stage_two(last - 2)
-        round_y(last - 2)
-        stage_two(last - 1)
-        round_y(last - 1)
-        b = take()
-        scores(last, b)
+        for i in (last - 2, last - 1):
+            stage_two(i)
+            round_y(i)
+        bk = take()
+        scores(last, bk)
         for u in range(2):
-            epilogue(split(span(y_split, last, 1))[:, u], natural(bank[b][:])[:, u], natural(compat_rows(last))[:, u])
-        result(last, b)
-        move(y_split, y_turned, last - 3, 2)
-        quantize_y(last - 3, 2)
-        store_codes(last - 3, 2)
-        move(y_split, y_turned, last - 1, 1)
-        move(y_split, y_turned, last, 1)
-        quantize_y(last - 1, 2)
-        store_codes(last - 1, 2)
-        store_scales(8, 4, (nc.sync, nc.scalar))
+            epilogue(split(span(y_split, last, 1))[:, u], natural(bank[bk][:])[:, u], natural(compat_rows(last))[:, u])
+        result(last, bk)
+        quantize_y(last - 5, 2)
+        store_codes(last - 5, 2)
+        for first in (last - 3, last - 1):
+            move(y_split, y_turned, first, 2)
+            quantize_y(first, 2)
+            store_codes(first, 2)
+        store_scales(6, 6, (nc.sync, nc.scalar))

@@ -193,11 +193,13 @@ def tile_triangle_label_scores_h1_kernel(
         make_identity(nc, ident[:])
         nc.vector.memset(b_scales[:].rearrange("p g n -> p (g n)").bitcast(U32), 0)
         nc.vector.memset(l_scales[:].rearrange("p g n -> p (g n)").bitcast(U32), 0)
-        load_a(0, slice(0, V))
-        load_a(1, slice(0, V))
-        load_scale_rows(b_scales, adj4_scales)
         for g in range(GROUPS):
-            load_b(g)
+            load_a(0, slice(g * K_PASS, (g + 1) * K_PASS))
+        load_scale_rows(b_scales, adj4_scales)
+        load_b(0)
+        load_a(1, slice(0, V))
+        load_b(1)
+        load_b(2)
         for i in range(2, 5):
             load_a(i, slice(0, V))
         load_scale_rows(l_scales, lab_scales)
@@ -228,16 +230,21 @@ def tile_triangle_label_scores_h1_kernel(
             result(i, b)
 
         warm_up(8)
-        split_a(nc.vector.tensor_copy, 0, 0, GROUPS)
-        split_a(nc.vector.tensor_copy, 1, 0, GROUPS)
-        for unit in units(a_at(0), 2 * GROUPS):
-            move(a_split, a_turned, *unit)
-            quantize_a(*unit)
+        for g in range(GROUPS):
+            split_a(nc.vector.tensor_copy, 0, g, 1)
+        for g in range(GROUPS):
+            move(a_split, a_turned, a_at(0) + g, 1)
+            quantize_a(a_at(0) + g, 1)
         warm_up(8)
+        split_a(nc.vector.tensor_copy, 1, 0, GROUPS)
         first_banks = [take() for n in range(GROUPS)]
         for g in range(GROUPS):
             for n in range(GROUPS):
                 path_pass(0, n, g, first_banks[n])
+            if g == 0:
+                for unit in units(a_at(1), GROUPS):
+                    move(a_split, a_turned, *unit)
+                    quantize_a(*unit)
         split_a(nc.scalar.copy, 2, 0, GROUPS)
         for n in range(GROUPS):
             triangles(0, n, first_banks[n])

from contextlib import ExitStack

import concourse.mybir as mybir
from concourse.masks import make_identity

V, C = 1536, 512
FLOPS = 2 * V * V * (V + C)

F32 = mybir.dt.float32
BF16 = mybir.dt.bfloat16
I32 = mybir.dt.int32
U32 = mybir.dt.uint32
U8 = mybir.dt.uint8
FP8X4 = mybir.dt.float8_e4m3fn_x4
FP4X4 = mybir.dt.float4_e2m1fn_x4
MULT = mybir.AluOpType.mult

P = 128
K_PASS = 512
GROUPS = V // K_PASS
TILES = V // P
RING = 4
R_BATCH = 4
HALF = 0.5


def tile_triangle_label_scores_h1_kernel(
    tc, adj, adj4_words, adj4_scales, lab_words, lab_scales, compat, out_0, out_1, out_2
):
    nc = tc.nc
    with ExitStack() as ctx:
        sb = ctx.enter_context(tc.tile_pool(name="sb", bufs=1))
        ps = ctx.enter_context(tc.psum_pool(name="ps", bufs=1))

        def sbuf(name, shape, dtype):
            return sb.tile(shape, dtype, name=name, align_bytes=64)

        ident = sbuf("ident", [P, P], F32)
        a_rows = [sbuf("a_rows%d" % i, [P, V], BF16) for i in range(TILES)]
        r_rows = [sbuf("r_rows%d" % k, [P, R_BATCH, C], BF16) for k in range(TILES // R_BATCH)]
        b_words = [sbuf("b_words%d" % g, [P, 2 * V], U8) for g in range(GROUPS)]
        b_scales = sbuf("b_scales", [P, GROUPS, V], U8)
        l_words = sbuf("l_words", [P, GROUPS, 2 * C], U8)
        l_scales = sbuf("l_scales", [P, GROUPS, C], U8)
        a_split = sbuf("a_split", [P, RING * V], BF16)
        a_turned = sbuf("a_turned", [P, RING * V], BF16)
        a_codes = sbuf("a_codes", [P, RING * GROUPS * P], U32)
        a_scales = sbuf("a_scales", [P, RING * GROUPS * P], U8)
        h_split = sbuf("h_split", [P, RING * V], BF16)
        h_turned = sbuf("h_turned", [P, RING * V], BF16)
        h_codes = sbuf("h_codes", [P, RING * GROUPS * P], U32)
        h_scales = sbuf("h_scales", [P, RING * GROUPS * P], U8)
        y_rows = sbuf("y_rows", [P, RING, C], F32)
        y_split = sbuf("y_split", [P, TILES * C], BF16)
        y_turned = sbuf("y_turned", [P, TILES * C], BF16)
        y_codes = sbuf("y_codes", [P, V], U32)
        y_scales = sbuf("y_scales", [P, V], U8)
        bank = [ps.tile([P, K_PASS], F32, name="bank%d" % b) for b in range(8)]
        taken = []

        def take():
            taken.append(len(taken) % 8)
            return taken[-1]

        ctx.enter_context(tc.manual_schedule())

        def natural(ap):
            return ap.rearrange("p (m u e) -> p u m e", u=2, e=2)

        def split(ap):
            return ap.rearrange("p (u m e) -> p u m e", u=2, e=2)

        def span(ap, first, count):
            return ap[:, first * K_PASS : (first + count) * K_PASS]

        def a_at(i):
            return (i + 1) % RING * GROUPS

        def h_at(i):
            return i % RING * GROUPS

        def load_a(i, cols):
            nc.sync.dma_start(out=a_rows[i][:, cols], in_=adj[i * P : (i + 1) * P, cols])

        def load_r(k):
            rows = compat[k * R_BATCH * P : (k + 1) * R_BATCH * P, :]
            nc.sync.dma_start(out=r_rows[k][:], in_=rows.rearrange("(s p) c -> p s c", p=P))

        def load_scale_rows(plane, rows):
            for q in range(4):
                nc.sync.dma_start(
                    out=plane[32 * q : 32 * q + 4, :, :].bitcast(I32),
                    in_=rows[:, 4 * q : 4 * q + 4, :].rearrange("g r n -> r g n").bitcast(I32),
                )

        def load_b(g):
            nc.sync.dma_start(out=b_words[g][:].bitcast(I32), in_=adj4_words[g].bitcast(I32))

        def split_a(copy, i, g, count):
            copy(
                out=span(a_split, a_at(i) + g, count).bitcast(F32).rearrange("p (g u m) -> p g u m", g=count, u=2),
                in_=span(a_rows[i], g, count).bitcast(F32).rearrange("p (g m u) -> p g u m", g=count, u=2),
            )

        def turn(src, first, count, b):
            words = span(src, first, count).bitcast(F32)
            for k in range(2 * count):
                cols = slice(k * P, (k + 1) * P)
                nc.tensor.transpose(bank[b][:, cols], words[:, cols], ident[:])

        def interleave(copy, dst, first, count, b):
            copy(
                out=span(dst, first, count).bitcast(F32).rearrange("p (g r u) -> p g r u", g=count, u=2),
                in_=bank[b][:, : count * 2 * P].rearrange("p (g u r) -> p g r u", g=count, u=2),
            )

        def quantize(codes, scales, turned, first, count):
            cols = slice(first * P, (first + count) * P)
            nc.vector.quantize_mx(
                out=codes[:, cols].bitcast(FP8X4), scales=scales[:, cols], in_=span(turned, first, count)
            )

        def quantize_a(first, count):
            quantize(a_codes, a_scales, a_turned, first, count)

        def quantize_h(first, count):
            quantize(h_codes, h_scales, h_turned, first, count)

        def quantize_y(first, count):
            quantize(y_codes, y_scales, y_turned, first, count)

        def mx_pass(b, codes, scales, at, g, words, word_scales):
            cols = slice((at + g) * P, (at + g + 1) * P)
            nc.tensor.matmul_mx(
                out=bank[b][:],
                lhsT=codes[:, cols].bitcast(FP8X4),
                lhsT_scale=scales[:, cols],
                rhs=words.bitcast(FP4X4),
                rhs_scale=word_scales,
                start=(g == 0),
                stop=(g == GROUPS - 1),
            )

        def path_pass(i, n, g, b):
            words = b_words[g][:, 2 * n * K_PASS : 2 * (n + 1) * K_PASS]
            mx_pass(b, a_codes, a_scales, a_at(i), g, words, span(b_scales[:, g, :], n, 1))

        def paths(i, n, b):
            for g in range(GROUPS):
                path_pass(i, n, g, b)

        def triangles(i, n, b):
            nc.vector.tensor_tensor(
                out=split(span(h_split, h_at(i) + n, 1)),
                in0=natural(bank[b][:]),
                in1=natural(span(a_rows[i], n, 1)),
                op=MULT,
            )

        def scores(i, b):
            for g in range(GROUPS):
                mx_pass(b, h_codes, h_scales, h_at(i), g, l_words[:, g, :], l_scales[:, g, :])

        def epilogue(out, sums, factors):
            nc.vector.scalar_tensor_tensor(out=out, in0=sums, scalar=HALF, in1=factors, op0=MULT, op1=MULT)

        def compat_rows(i):
            return r_rows[i // R_BATCH][:, i % R_BATCH, :]

        def result(i, b):
            epilogue(y_rows[:, i % RING, :], bank[b][:], compat_rows(i))
            nc.sync.dma_start(out=out_0[i * P : (i + 1) * P, :], in_=y_rows[:, i % RING, :])

        def round_y(i):
            nc.scalar.copy(out=split(span(y_split, i, 1)), in_=natural(y_rows[:, i % RING, :]))

        def store_codes(first, count):
            cols = slice(first * P, (first + count) * P)
            words = out_1[0].rearrange("p m t -> p (m t)").bitcast(I32)
            nc.sync.dma_start(out=words[:, cols], in_=y_codes[:, cols].bitcast(I32))

        def store_scales(first, count, queues):
            cols = slice(first * P // 4, (first + count) * P // 4)
            rows = out_2[0].bitcast(I32)
            for q in range(4):
                live = y_scales[32 * q : 32 * q + 4, :].bitcast(I32)
                queues[q % 2].dma_start(out=rows[4 * q : 4 * q + 4, cols], in_=live[:, cols])

        def warm_up(count):
            for k in range(count):
                nc.tensor.transpose(bank[7][:, (k % 4) * P : (k % 4 + 1) * P], ident[:], ident[:])

        make_identity(nc, ident[:])
        nc.vector.memset(b_scales[:].rearrange("p g n -> p (g n)").bitcast(U32), 0)
        nc.vector.memset(l_scales[:].rearrange("p g n -> p (g n)").bitcast(U32), 0)
        for g in range(GROUPS):
            load_a(0, slice(g * K_PASS, (g + 1) * K_PASS))
        load_scale_rows(b_scales, adj4_scales)
        load_b(0)
        load_a(1, slice(0, V))
        load_b(1)
        load_b(2)
        for i in range(2, 5):
            load_a(i, slice(0, V))
        load_scale_rows(l_scales, lab_scales)
        nc.sync.dma_start(out=l_words[:].bitcast(I32), in_=lab_words.rearrange("g p b -> p g b").bitcast(I32))
        load_r(0)
        for i in range(5, TILES):
            load_a(i, slice(0, V))
            if i % R_BATCH == 3:
                load_r(i // R_BATCH)

        def units(first, count):
            odd = [(first, 1)] if count % 2 else []
            return odd + [(k, 2) for k in range(first + count % 2, first + count, 2)]

        def move(src, dst, first, count, copy=nc.scalar.copy):
            b = take()
            turn(src, first, count, b)
            interleave(copy, dst, first, count, b)

        def stage_one(i, n):
            b = take()
            paths(i, n, b)
            triangles(i, n, b)

        def stage_two(i):
            b = take()
            scores(i, b)
            result(i, b)

        warm_up(8)
        for g in range(GROUPS):
            split_a(nc.vector.tensor_copy, 0, g, 1)
        for g in range(GROUPS):
            move(a_split, a_turned, a_at(0) + g, 1)
            quantize_a(a_at(0) + g, 1)
        warm_up(8)
        split_a(nc.vector.tensor_copy, 1, 0, GROUPS)
        first_banks = [take() for n in range(GROUPS)]
        for g in range(GROUPS):
            for n in range(GROUPS):
                path_pass(0, n, g, first_banks[n])
            if g == 0:
                for unit in units(a_at(1), GROUPS):
                    move(a_split, a_turned, *unit)
                    quantize_a(*unit)
        split_a(nc.scalar.copy, 2, 0, GROUPS)
        for n in range(GROUPS):
            triangles(0, n, first_banks[n])
        split_a(nc.scalar.copy, 3, 0, GROUPS)
        split_a(nc.scalar.copy, 4, 0, GROUPS)
        for n in range(GROUPS):
            stage_one(1, n)

        last = TILES - 1
        for a in range(2, TILES, 2):
            b = a + 1
            a_units = units(a_at(b), GROUPS * (2 if b < last else 1))
            if a == 2:
                a_units = units(a_at(a), GROUPS) + a_units
            h_units = units(h_at(a - 2), 2 * GROUPS)
            for unit in a_units:
                move(a_split, a_turned, *unit)
                quantize_a(*unit)
            for unit in h_units:
                move(h_split, h_turned, *unit)
            if a >= 6:
                move(y_split, y_turned, a - 6, 2)
            for i in range(b + 2, min(b + 4, TILES)):
                split_a(nc.scalar.copy, i, 0, GROUPS)
            if a >= 4:
                round_y(a - 4)
                round_y(b - 4)
            waiting = [(quantize_h, unit) for unit in h_units]
            if a >= 6:
                waiting = waiting + [(quantize_y, (a - 6, 2))]
            for k in range(2 * GROUPS):
                bk = take()
                paths(a + k // GROUPS, k % GROUPS, bk)
                for job, unit in waiting[k : k + 1]:
                    job(*unit)
                triangles(a + k // GROUPS, k % GROUPS, bk)
            if a >= 6:
                store_codes(a - 6, 2)
            stage_two(a - 2)
            if b < last:
                stage_two(b - 2)

        store_scales(0, 6, (nc.sync, nc.sync))
        for unit in units(h_at(last - 1), 2 * GROUPS):
            move(h_split, h_turned, *unit)
            quantize_h(*unit)
        move(y_split, y_turned, last - 5, 2)
        round_y(last - 3)
        for i in (last - 2, last - 1):
            stage_two(i)
            round_y(i)
        bk = take()
        scores(last, bk)
        for u in range(2):
            epilogue(split(span(y_split, last, 1))[:, u], natural(bank[bk][:])[:, u], natural(compat_rows(last))[:, u])
        result(last, bk)
        quantize_y(last - 5, 2)
        store_codes(last - 5, 2)
        for first in (last - 3, last - 1):
            move(y_split, y_turned, first, 2)
            quantize_y(first, 2)
            store_codes(first, 2)
        store_scales(6, 6, (nc.sync, nc.scalar))
